import numpy as np
import ml_dtypes


def mxq(x, axis, fmt="e4m3"):
    dtype, down = {"e4m3": (ml_dtypes.float8_e4m3fn, 7), "e5m2": (ml_dtypes.float8_e5m2, 14)}[fmt]
    v = np.moveaxis(np.asarray(x, np.float32).astype(ml_dtypes.bfloat16).astype(np.float64), axis, -1)
    blocks = v.reshape(v.shape[:-1] + (-1, 32))
    amax = np.abs(blocks).max(-1, keepdims=True)
    byte = np.maximum(np.where(amax > 0, np.frexp(amax)[1] - 1 + 127, 0) - down, 1)
    scale = np.exp2(byte - 127.0)
    codes = (blocks / scale).astype(np.float32).astype(dtype).astype(np.float64)
    return np.moveaxis((codes * scale).reshape(v.shape), -1, axis)


WIDE = False


def mx_kscale(k):
    if not WIDE:
        return np.ones(k)
    levels = np.array([10, -10, 5, -5, 0])
    if k % 512:
        return np.exp2(np.random.permutation(np.resize(levels, k // 32))).repeat(32)
    a = np.empty((k // 512, 16))
    for p in range(k // 512):
        a[p, :8] = np.random.permutation(np.resize(levels, 8))
        for g in range(8):
            far = levels[np.abs(levels - a[p, g]) >= 10]
            a[p, g + 8] = far[np.random.randint(len(far))]
    return np.exp2(a.ravel()).repeat(32)


def f64(x):
    return np.asarray(x).astype(np.float64)


def striped(idx):
    return np.tile(idx.reshape(-1, 16).T, (8, 1)).astype(np.uint16)


def unstriped(offs):
    return offs[:16].T.reshape(-1).astype(np.int64)


def relu(v):
    return np.maximum(v, 0.0)


K, T, S, H, N = 512, 1024, 512, 1024, 512


def setup_inputs():
    n = np.random.standard_normal
    s = mx_kscale(K)[:, None]
    u = mx_kscale(H)
    return {
        "xT": (n((K, T)) * s).astype(np.float32),
        "w1": (n((K, H)) / np.sqrt(K) / s).astype(np.float32),
        "w3": (n((K, H)) / np.sqrt(K) / s * u).astype(np.float32),
        "w2": (n((H, N)) / np.sqrt(H) / u[:, None]).astype(np.float32),
        "offs": striped(np.sort(np.random.permutation(T)[:S])),
    }


def reference(xT, w1, w3, w2, offs):
    idx = unstriped(offs)
    xq = mxq(f64(xT)[:, idx], 0, "e4m3")
    h = relu(mxq(f64(w1), 0, "e4m3").T @ xq) * (mxq(f64(w3), 0, "e4m3").T @ xq)
    y = mxq(f64(w2), 0, "e4m3").T @ mxq(h, 0, "e4m3")
    return y

@@ -1,0 +1,198 @@
+from contextlib import ExitStack
+
+import concourse.mybir as mybir
+
+K, T, S, H, N = 512, 1024, 512, 1024, 512
+FLOPS = 2 * S * (2 * K * H + H * N)
+
+F32 = mybir.dt.float32
+BF16 = mybir.dt.bfloat16
+U32 = mybir.dt.uint32
+U16 = mybir.dt.uint16
+U8 = mybir.dt.uint8
+FP8X4 = mybir.dt.float8_e4m3fn_x4
+ADD = mybir.AluOpType.add
+MULT = mybir.AluOpType.mult
+RELU = mybir.ActivationFunctionType.Relu
+
+P = 128
+J = 4
+KP = P * J
+NB = 128
+
+ORDER = [["x",0,512],["x",512,512],["a",0,256],["a",256,256],["b",0,256],["b",256,256],["c",0,256],["a",512,256],["a",768,256],["b",512,256],["b",768,256],["d",0,256],["c",256,256],["d",256,256]]
+SPLIT = {"x0":[["V",320],["S",192]],"x512":[["V",352],["S",160]],"a0":[["V",64],["S",192]],"a256":[["S",256]],"b0":[["V",64],["S",192]],"b256":[["V",192],["S",64]],"a512":[["V",96],["S",160]],"a768":[["S",256]],"b512":[["S",256]],"b768":[["V",160],["S",96]],"c0":[["V",256]],"d0":[["V",32],["S",224]],"c256":[["V",160],["S",96]],"d256":[["S",256]]}
+H_GROUP = [4,2]
+OUT_ENGINES = "SVSV"
+
+
+def tile_picked_pick_glu_relu_srt_e_kernel(tc, xT, w1, w3, w2, offs, out):
+    nc = tc.nc
+
+    def copy(engine, dst, src):
+        if engine == "V":
+            nc.vector.tensor_copy(out=dst, in_=src)
+        elif engine == "S":
+            nc.scalar.copy(out=dst, in_=src)
+        else:
+            nc.gpsimd.tensor_scalar(out=dst, in0=src, scalar1=1.0, scalar2=0.0, op0=MULT, op1=ADD)
+
+    with ExitStack() as ctx:
+        keep = ctx.enter_context(tc.tile_pool(name="keep", bufs=1))
+        psum = ctx.enter_context(tc.psum_pool(name="psum", bufs=8))
+
+        offsets = keep.tile([P, S // 16], U16, name="offsets")
+        sources = {
+            "x": xT.rearrange("(p j) w -> p j w", j=J),
+            "a": w1.rearrange("(p j) w -> p j w", j=J),
+            "b": w3.rearrange("(p j) w -> p j w", j=J),
+            "c": w2[:KP, :].rearrange("(p j) w -> p j w", j=J),
+            "d": w2[KP:, :].rearrange("(p j) w -> p j w", j=J),
+        }
+        raws = {}
+        pieces = {}
+        for i, (key, first, width) in enumerate(ORDER):
+            raw = keep.tile([P, J, width], F32, name=f"raw_{key}_{first}")
+            nc.sync.dma_start(out=raw[:], in_=sources[key][:, :, first : first + width])
+            raws[(key, first)] = raw
+            if i == 0:
+                nc.sync.dma_start(offsets[:], offs)
+
+        x_codes = keep.tile([P, T], U32, name="x_codes", align_bytes=64)
+        x_scales = keep.tile([P, T], U8, name="x_scales", align_bytes=64)
+        nc.gpsimd.memset(x_scales[:], 0)
+        xg_codes = keep.tile([P, S], U32, name="xg_codes", align_bytes=64)
+        xg_scales = keep.tile([P, S], U8, name="xg_scales", align_bytes=64)
+
+        for key, first, width in ORDER:
+            if key == "x":
+                raw = raws[(key, first)]
+                grouped = keep.tile([P, width, J], BF16, name=f"x_grouped{first}", align_bytes=64)
+                a = 0
+                for engine, n in SPLIT[f"{key}{first}"]:
+                    copy(
+                        engine,
+                        grouped[:, a : a + n, :].rearrange("p (c i) j -> p c j i", i=4),
+                        raw[:, :, a : a + n].rearrange("p j (c i) -> p c j i", i=4),
+                    )
+                    a += n
+                nc.vector.quantize_mx(
+                    out=x_codes[:, first : first + width].bitcast(FP8X4),
+                    scales=x_scales[:, first : first + width],
+                    in_=grouped[:].rearrange("p w j -> p (w j)"),
+                )
+        nc.vector.tensor_copy(xg_codes[:], x_codes[:].indirect(offsets[:]))
+        nc.vector.tensor_copy(xg_scales[:], x_scales[:].indirect(offsets[:]))
+
+        w_codes = {}
+        w_scales = {}
+
+        def first_weights(w, c):
+            grouped = keep.tile([P, J, P, J], BF16, name=f"w_grouped_{w}{c}", align_bytes=64)
+            codes = keep.tile([P, KP], U32, name=f"w_codes_{w}{c}", align_bytes=64)
+            scales = keep.tile([P, KP], U8, name=f"w_scales_{w}{c}", align_bytes=64)
+            for key, first, width in ORDER:
+                if key == w and first // KP == c:
+                    raw = raws[(key, first)]
+                    m0 = (first - c * KP) // 4
+                    a = 0
+                    for engine, n in SPLIT[f"{key}{first}"]:
+                        b = a + n
+                        copy(
+                            engine,
+                            grouped[:, :, m0 + a // 4 : m0 + b // 4, :].rearrange("p t m j -> p m t j"),
+                            raw[:, :, a:b].rearrange("p j (m t) -> p m t j", t=4),
+                        )
+                        a = b
+            nc.vector.quantize_mx(
+                out=codes[:].bitcast(FP8X4), scales=scales[:], in_=grouped[:].rearrange("p t m j -> p (t m j)")
+            )
+            w_codes[(w, c)] = codes
+            w_scales[(w, c)] = scales
+
+        h_codes = []
+        h_scales = []
+
+        def products(w, c, b):
+            cols = slice(b * NB, (b + 1) * NB)
+            bank = psum.tile([P, J, NB], F32, name="bank", tag="bank")
+            for t in range(J):
+                rows = slice(t * P, (t + 1) * P)
+                nc.tensor.matmul_mx(
+                    out=bank[:, t, :],
+                    lhsT=w_codes[(w, c)][:, rows].bitcast(FP8X4),
+                    lhsT_scale=w_scales[(w, c)][:, rows],
+                    rhs=xg_codes[:, cols].bitcast(FP8X4),
+                    rhs_scale=xg_scales[:, cols],
+                    start=True,
+                    stop=True,
+                )
+            return bank[:].rearrange("p t n -> p n t")
+
+        def first_layer(c):
+            grouped = keep.tile([P, S, J], BF16, name=f"h_grouped{c}", align_bytes=64)
+            codes = keep.tile([P, S], U32, name=f"h_codes{c}", align_bytes=64)
+            scales = keep.tile([P, S], U8, name=f"h_scales{c}", align_bytes=64)
+            gates = []
+            for b in range(S // NB):
+                gate = keep.tile([P, NB, J], F32, name=f"gate{c}_{b}")
+                nc.scalar.activation(gate[:], products("a", c, b), RELU)
+                gates.append(gate)
+            for b in range(S // NB):
+                up = products("b", c, b)
+                nc.vector.tensor_tensor(
+                    out=grouped[:, b * NB : (b + 1) * NB, :], in0=gates[b][:], in1=up, op=MULT
+                )
+                if (b + 1) % H_GROUP[c] == 0:
+                    cols = slice((b + 1 - H_GROUP[c]) * NB, (b + 1) * NB)
+                    nc.vector.quantize_mx(
+                        out=codes[:, cols].bitcast(FP8X4),
+                        scales=scales[:, cols],
+                        in_=grouped[:, cols, :].rearrange("p n j -> p (n j)"),
+                    )
+            h_codes.append(codes)
+            h_scales.append(scales)
+
+        for c in range(2):
+            first_weights("a", c)
+            first_weights("b", c)
+            first_layer(c)
+
+        for half in [0,1]:
+            w2_codes = []
+            w2_scales = []
+            for key in ("c", "d"):
+                grouped = keep.tile([P, 256, J], BF16, name=f"w2_grouped_{key}{half}", align_bytes=64)
+                codes = keep.tile([P, 256], U32, name=f"w2_codes_{key}{half}", align_bytes=64)
+                scales = keep.tile([P, 256], U8, name=f"w2_scales_{key}{half}", align_bytes=64)
+                raw = raws[(key, half * 256)]
+                a = 0
+                for engine, n in SPLIT[f"{key}{half * 256}"]:
+                    copy(
+                        engine,
+                        grouped[:, a : a + n, :].rearrange("p (c i) j -> p c j i", i=4),
+                        raw[:, :, a : a + n].rearrange("p j (c i) -> p c j i", i=4),
+                    )
+                    a += n
+                nc.vector.quantize_mx(
+                    out=codes[:].bitcast(FP8X4), scales=scales[:], in_=grouped[:].rearrange("p m j -> p (m j)")
+                )
+                w2_codes.append(codes)
+                w2_scales.append(scales)
+            for q in range(2):
+                rows = slice(q * P, (q + 1) * P)
+                bank = psum.tile([P, S], F32, name="bank", tag="bank")
+                for c in range(2):
+                    nc.tensor.matmul_mx(
+                        out=bank[:],
+                        lhsT=w2_codes[c][:, rows].bitcast(FP8X4),
+                        lhsT_scale=w2_scales[c][:, rows],
+                        rhs=h_codes[c][:].bitcast(FP8X4),
+                        rhs_scale=h_scales[c][:],
+                        start=(c == 0),
+                        stop=(c == 1),
+                    )
+                result = keep.tile([P, S], F32, name=f"result{half}_{q}")
+                copy(OUT_ENGINES[2 * half + q], result[:], bank[:])
+                m0 = half * 256 + q * P
+                nc.sync.dma_start(out=out[m0 : m0 + P, :], in_=result[:])

@@ -20,10 +20,10 @@ J = 4
 KP = P * J
 NB = 128
 
-ORDER = [["x",0,512],["x",512,512],["a",0,256],["a",256,256],["b",0,256],["b",256,256],["c",0,256],["a",512,256],["a",768,256],["b",512,256],["b",768,256],["d",0,256],["c",256,256],["d",256,256]]
-SPLIT = {"x0":[["V",320],["S",192]],"x512":[["V",352],["S",160]],"a0":[["V",64],["S",192]],"a256":[["S",256]],"b0":[["V",64],["S",192]],"b256":[["V",192],["S",64]],"a512":[["V",96],["S",160]],"a768":[["S",256]],"b512":[["S",256]],"b768":[["V",160],["S",96]],"c0":[["V",256]],"d0":[["V",32],["S",224]],"c256":[["V",160],["S",96]],"d256":[["S",256]]}
-H_GROUP = [4,2]
-OUT_ENGINES = "SVSV"
+ORDER = [["x",0,512],["x",512,512],["a",0,512],["b",0,512],["a",512,512],["b",512,512],["c",0,512],["d",0,512]]
+SPLIT = {"x0":[["V",512]],"x512":[["V",320],["S",192]],"a0":[["V",192],["S",64]],"a256":[["S",256]],"b0":[["V",64],["S",192]],"b256":[["V",256]],"a512":[["S",256]],"a768":[["V",192],["S",64]],"b512":[["V",128],["S",128]],"b768":[["S",256]],"c0":[["V",192],["S",64]],"d0":[["S",256]],"c256":[["V",192],["S",64]],"d256":[["S",256]]}
+H_GROUP = [2,4]
+OUT_ENGINES = "VSVV"
 
 
 def tile_picked_pick_glu_relu_srt_e_kernel(tc, xT, w1, w3, w2, offs, out):
@@ -46,15 +46,20 @@ def tile_picked_pick_glu_relu_srt_e_kernel(tc, xT, w1, w3, w2, offs, out):
             "x": xT.rearrange("(p j) w -> p j w", j=J),
             "a": w1.rearrange("(p j) w -> p j w", j=J),
             "b": w3.rearrange("(p j) w -> p j w", j=J),
-            "c": w2[:KP, :].rearrange("(p j) w -> p j w", j=J),
-            "d": w2[KP:, :].rearrange("(p j) w -> p j w", j=J),
+            "c": w2[:KP, :].rearrange("(g t b) m -> t g b m", t=4, b=4),
+            "d": w2[KP:, :].rearrange("(g t b) m -> t g b m", t=4, b=4),
         }
         raws = {}
-        pieces = {}
         for i, (key, first, width) in enumerate(ORDER):
             raw = keep.tile([P, J, width], F32, name=f"raw_{key}_{first}")
-            nc.sync.dma_start(out=raw[:], in_=sources[key][:, :, first : first + width])
-            raws[(key, first)] = raw
+            if key in "cd":
+                for t in range(4):
+                    nc.sync.dma_start(out=raw[:, t, :], in_=sources[key][t, :, :, first : first + width])
+            else:
+                nc.sync.dma_start(out=raw[:], in_=sources[key][:, :, first : first + width])
+            step = 512 if key == "x" else 256
+            for sub in range(0, width, step):
+                raws[(key, first + sub)] = raw[:, :, sub : sub + step]
             if i == 0:
                 nc.sync.dma_start(offsets[:], offs)
 
@@ -91,8 +96,9 @@ def tile_picked_pick_glu_relu_srt_e_kernel(tc, xT, w1, w3, w2, offs, out):
             grouped = keep.tile([P, J, P, J], BF16, name=f"w_grouped_{w}{c}", align_bytes=64)
             codes = keep.tile([P, KP], U32, name=f"w_codes_{w}{c}", align_bytes=64)
             scales = keep.tile([P, KP], U8, name=f"w_scales_{w}{c}", align_bytes=64)
-            for key, first, width in ORDER:
-                if key == w and first // KP == c:
+            for first in (c * KP, c * KP + 256):
+                if True:
+                    key = w
                     raw = raws[(key, first)]
                     m0 = (first - c * KP) // 4
                     a = 0
@@ -100,8 +106,8 @@ def tile_picked_pick_glu_relu_srt_e_kernel(tc, xT, w1, w3, w2, offs, out):
                         b = a + n
                         copy(
                             engine,
-                            grouped[:, :, m0 + a // 4 : m0 + b // 4, :].rearrange("p t m j -> p m t j"),
-                            raw[:, :, a:b].rearrange("p j (m t) -> p m t j", t=4),
+                            grouped[:, :, m0 + a // 4 : m0 + b // 4, :].rearrange("p t (g b) j -> p g t j b", b=4),
+                            raw[:, :, a:b].rearrange("p j (g t b) -> p g t j b", t=4, b=4),
                         )
                         a = b
             nc.vector.quantize_mx(

@@ -19,11 +19,16 @@ P = 128
 J = 4
 KP = P * J
 NB = 128
+Q = 256
 
-ORDER = [["x",0,512],["x",512,512],["a",0,512],["b",0,512],["a",512,512],["b",512,512],["c",0,512],["d",0,512]]
-SPLIT = {"x0":[["V",512]],"x512":[["V",320],["S",192]],"a0":[["V",192],["S",64]],"a256":[["S",256]],"b0":[["V",64],["S",192]],"b256":[["V",256]],"a512":[["S",256]],"a768":[["V",192],["S",64]],"b512":[["V",128],["S",128]],"b768":[["S",256]],"c0":[["V",192],["S",64]],"d0":[["S",256]],"c256":[["V",192],["S",64]],"d256":[["S",256]]}
-H_GROUP = [2,4]
-OUT_ENGINES = "VSVV"
+ORDER = [["x",0,512],["x",512,512],["a",0,512],["b",0,512],["a",512,512],["b",512,256],["b",768,256],["c",0,512],["d",0,256],["d",256,256]]
+SPLIT = {"x0":[["V",160],["S",96]],"x256":[["V",128],["S",128]],"x512":[["S",256]],"x768":[["V",256]],"a0":[["V",160],["S",96]],"a256":[["S",256]],"b0":[["V",192],["S",64]],"b256":[["S",256]],"a512":[["V",256]],"a768":[["V",224],["S",32]],"b512":[["V",64],["S",192]],"b768":[["S",256]],"c0":[["S",256]],"c256":[["V",96],["S",32]],"c384":[["S",128]],"d0":[["S",256]],"d256":[["S",128]],"d384":[["V",128]]}
+STAGES = ["d0","b1","a0","c0","b0","x","a1","h0","h1","c1","d1","d2","c2"]
+H_GROUP = [4,2]
+X_QUANT = [[0,512],[512,256],[768,256]]
+W2_QUANT = [[0,256],[256,128],[384,128]]
+L2 = [[[0,1,2,"S"]],[[1,0,2,"S"]],[[1,1,2,"V"]],[[0,0,2,"S"]],[[2,0,2,"S"]],[[2,1,2,"V"]],[[3,0,2,"V"]],[[3,1,2,"S"]]]
+G_STEP = 256
 
 
 def tile_picked_pick_glu_relu_srt_e_kernel(tc, xT, w1, w3, w2, offs, out):
@@ -46,20 +51,15 @@ def tile_picked_pick_glu_relu_srt_e_kernel(tc, xT, w1, w3, w2, offs, out):
             "x": xT.rearrange("(p j) w -> p j w", j=J),
             "a": w1.rearrange("(p j) w -> p j w", j=J),
             "b": w3.rearrange("(p j) w -> p j w", j=J),
-            "c": w2[:KP, :].rearrange("(g t b) m -> t g b m", t=4, b=4),
-            "d": w2[KP:, :].rearrange("(g t b) m -> t g b m", t=4, b=4),
+            "c": w2[:KP, :].rearrange("(p j) w -> p j w", j=J),
+            "d": w2[KP:, :].rearrange("(p j) w -> p j w", j=J),
         }
         raws = {}
         for i, (key, first, width) in enumerate(ORDER):
             raw = keep.tile([P, J, width], F32, name=f"raw_{key}_{first}")
-            if key in "cd":
-                for t in range(4):
-                    nc.sync.dma_start(out=raw[:, t, :], in_=sources[key][t, :, :, first : first + width])
-            else:
-                nc.sync.dma_start(out=raw[:], in_=sources[key][:, :, first : first + width])
-            step = 512 if key == "x" else 256
-            for sub in range(0, width, step):
-                raws[(key, first + sub)] = raw[:, :, sub : sub + step]
+            nc.sync.dma_start(out=raw[:], in_=sources[key][:, :, first : first + width])
+            for sub in range(0, width, 128):
+                raws[(key, first + sub)] = (raw, sub)
             if i == 0:
                 nc.sync.dma_start(offsets[:], offs)
 
@@ -69,25 +69,37 @@ def tile_picked_pick_glu_relu_srt_e_kernel(tc, xT, w1, w3, w2, offs, out):
         xg_codes = keep.tile([P, S], U32, name="xg_codes", align_bytes=64)
         xg_scales = keep.tile([P, S], U8, name="xg_scales", align_bytes=64)
 
-        for key, first, width in ORDER:
-            if key == "x":
-                raw = raws[(key, first)]
+        def shares(key, first):
+            found = []
+            a = 0
+            for engine, n in SPLIT[f"{key}{first}"]:
+                step = G_STEP if engine == "G" else n
+                for s in range(0, n, step):
+                    found.append((engine, a + s, a + min(s + step, n)))
+                a += n
+            return found
+
+        def plain_casts(key, first, grouped):
+            for engine, a, b in shares(key, first):
+                raw, sub = raws[(key, first)]
+                copy(
+                    engine,
+                    grouped[:, a:b, :].rearrange("p (c i) j -> p c j i", i=4),
+                    raw[:, :, sub + a : sub + b].rearrange("p j (c i) -> p c j i", i=4),
+                )
+
+        def tokens():
+            for first, width in X_QUANT:
                 grouped = keep.tile([P, width, J], BF16, name=f"x_grouped{first}", align_bytes=64)
-                a = 0
-                for engine, n in SPLIT[f"{key}{first}"]:
-                    copy(
-                        engine,
-                        grouped[:, a : a + n, :].rearrange("p (c i) j -> p c j i", i=4),
-                        raw[:, :, a : a + n].rearrange("p j (c i) -> p c j i", i=4),
-                    )
-                    a += n
+                for sub in range(0, width, Q):
+                    plain_casts("x", first + sub, grouped[:, sub : sub + Q, :])
                 nc.vector.quantize_mx(
                     out=x_codes[:, first : first + width].bitcast(FP8X4),
                     scales=x_scales[:, first : first + width],
                     in_=grouped[:].rearrange("p w j -> p (w j)"),
                 )
-        nc.vector.tensor_copy(xg_codes[:], x_codes[:].indirect(offsets[:]))
-        nc.vector.tensor_copy(xg_scales[:], x_scales[:].indirect(offsets[:]))
+            nc.vector.tensor_copy(xg_codes[:], x_codes[:].indirect(offsets[:]))
+            nc.vector.tensor_copy(xg_scales[:], x_scales[:].indirect(offsets[:]))
 
         w_codes = {}
         w_scales = {}
@@ -96,28 +108,23 @@ def tile_picked_pick_glu_relu_srt_e_kernel(tc, xT, w1, w3, w2, offs, out):
             grouped = keep.tile([P, J, P, J], BF16, name=f"w_grouped_{w}{c}", align_bytes=64)
             codes = keep.tile([P, KP], U32, name=f"w_codes_{w}{c}", align_bytes=64)
             scales = keep.tile([P, KP], U8, name=f"w_scales_{w}{c}", align_bytes=64)
-            for first in (c * KP, c * KP + 256):
-                if True:
-                    key = w
-                    raw = raws[(key, first)]
-                    m0 = (first - c * KP) // 4
-                    a = 0
-                    for engine, n in SPLIT[f"{key}{first}"]:
-                        b = a + n
-                        copy(
-                            engine,
-                            grouped[:, :, m0 + a // 4 : m0 + b // 4, :].rearrange("p t (g b) j -> p g t j b", b=4),
-                            raw[:, :, a:b].rearrange("p j (g t b) -> p g t j b", t=4, b=4),
-                        )
-                        a = b
+            for sub in (0, Q):
+                raw, at = raws[(w, c * KP + sub)]
+                m0 = sub // 4
+                for engine, a, b in shares(w, c * KP + sub):
+                    copy(
+                        engine,
+                        grouped[:, :, m0 + a // 4 : m0 + b // 4, :].rearrange("p t m j -> p m t j"),
+                        raw[:, :, at + a : at + b].rearrange("p j (m t) -> p m t j", t=4),
+                    )
             nc.vector.quantize_mx(
                 out=codes[:].bitcast(FP8X4), scales=scales[:], in_=grouped[:].rearrange("p t m j -> p (t m j)")
             )
             w_codes[(w, c)] = codes
             w_scales[(w, c)] = scales
 
-        h_codes = []
-        h_scales = []
+        h_codes = {}
+        h_scales = {}
 
         def products(w, c, b):
             cols = slice(b * NB, (b + 1) * NB)
@@ -156,49 +163,54 @@ def tile_picked_pick_glu_relu_srt_e_kernel(tc, xT, w1, w3, w2, offs, out):
                         scales=scales[:, cols],
                         in_=grouped[:, cols, :].rearrange("p n j -> p (n j)"),
                     )
-            h_codes.append(codes)
-            h_scales.append(scales)
+            h_codes[c] = codes
+            h_scales[c] = scales
 
-        for c in range(2):
-            first_weights("a", c)
-            first_weights("b", c)
-            first_layer(c)
+        w2_codes = {}
+        w2_scales = {}
 
-        for half in [0,1]:
-            w2_codes = []
-            w2_scales = []
-            for key in ("c", "d"):
-                grouped = keep.tile([P, 256, J], BF16, name=f"w2_grouped_{key}{half}", align_bytes=64)
-                codes = keep.tile([P, 256], U32, name=f"w2_codes_{key}{half}", align_bytes=64)
-                scales = keep.tile([P, 256], U8, name=f"w2_scales_{key}{half}", align_bytes=64)
-                raw = raws[(key, half * 256)]
-                a = 0
-                for engine, n in SPLIT[f"{key}{half * 256}"]:
-                    copy(
-                        engine,
-                        grouped[:, a : a + n, :].rearrange("p (c i) j -> p c j i", i=4),
-                        raw[:, :, a : a + n].rearrange("p j (c i) -> p c j i", i=4),
-                    )
-                    a += n
-                nc.vector.quantize_mx(
-                    out=codes[:].bitcast(FP8X4), scales=scales[:], in_=grouped[:].rearrange("p m j -> p (m j)")
-                )
-                w2_codes.append(codes)
-                w2_scales.append(scales)
-            for q in range(2):
-                rows = slice(q * P, (q + 1) * P)
-                bank = psum.tile([P, S], F32, name="bank", tag="bank")
-                for c in range(2):
+        def second_weights(key, piece):
+            first, width = W2_QUANT[piece]
+            grouped = keep.tile([P, width, J], BF16, name=f"w2_grouped_{key}{piece}", align_bytes=64)
+            codes = keep.tile([P, width], U32, name=f"w2_codes_{key}{piece}", align_bytes=64)
+            scales = keep.tile([P, width], U8, name=f"w2_scales_{key}{piece}", align_bytes=64)
+            plain_casts(key, first, grouped)
+            nc.vector.quantize_mx(
+                out=codes[:].bitcast(FP8X4), scales=scales[:], in_=grouped[:].rearrange("p m j -> p (m j)")
+            )
+            for m in range(0, width, P):
+                w2_codes[(key, (first + m) // P)] = codes[:, m : m + P]
+                w2_scales[(key, (first + m) // P)] = scales[:, m : m + P]
+
+        for stage in STAGES:
+            if stage == "x":
+                tokens()
+            elif stage[0] in "ab":
+                first_weights(stage[0], int(stage[1]))
+            elif stage[0] == "h":
+                first_layer(int(stage[1]))
+            else:
+                second_weights(stage[0], int(stage[1]))
+
+        for group in L2:
+            banks = []
+            for m, th, parts, engine in group:
+                bank = psum.tile([P, S // parts], F32, name="bank", tag="bank")
+                banks.append(bank)
+            for c, key in enumerate("cd"):
+                for bank, (m, th, parts, engine) in zip(banks, group):
+                    cols = slice(th * (S // parts), (th + 1) * (S // parts))
                     nc.tensor.matmul_mx(
                         out=bank[:],
-                        lhsT=w2_codes[c][:, rows].bitcast(FP8X4),
-                        lhsT_scale=w2_scales[c][:, rows],
-                        rhs=h_codes[c][:].bitcast(FP8X4),
-                        rhs_scale=h_scales[c][:],
+                        lhsT=w2_codes[(key, m)].bitcast(FP8X4),
+                        lhsT_scale=w2_scales[(key, m)],
+                        rhs=h_codes[c][:, cols].bitcast(FP8X4),
+                        rhs_scale=h_scales[c][:, cols],
                         start=(c == 0),
                         stop=(c == 1),
                     )
-                result = keep.tile([P, S], F32, name=f"result{half}_{q}")
-                copy(OUT_ENGINES[2 * half + q], result[:], bank[:])
-                m0 = half * 256 + q * P
-                nc.sync.dma_start(out=out[m0 : m0 + P, :], in_=result[:])
+            for bank, (m, th, parts, engine) in zip(banks, group):
+                cols = slice(th * (S // parts), (th + 1) * (S // parts))
+                result = keep.tile([P, S // parts], F32, name=f"result{m}_{th}")
+                copy(engine, result[:], bank[:])
+                nc.sync.dma_start(out=out[m * P : (m + 1) * P, cols], in_=result[:])

from contextlib import ExitStack

import concourse.mybir as mybir

K, T, S, H, N = 512, 1024, 512, 1024, 512
FLOPS = 2 * S * (2 * K * H + H * N)

F32 = mybir.dt.float32
BF16 = mybir.dt.bfloat16
U32 = mybir.dt.uint32
U16 = mybir.dt.uint16
U8 = mybir.dt.uint8
FP8X4 = mybir.dt.float8_e4m3fn_x4
ADD = mybir.AluOpType.add
MULT = mybir.AluOpType.mult
RELU = mybir.ActivationFunctionType.Relu

P = 128
J = 4
KP = P * J
NB = 128
Q = 256

ORDER = [["x",0,512],["x",512,512],["a",0,512],["b",0,512],["a",512,512],["b",512,256],["b",768,256],["c",0,512],["d",0,256],["d",256,256]]
SPLIT = {"x0":[["V",160],["S",96]],"x256":[["V",128],["S",128]],"x512":[["S",256]],"x768":[["V",256]],"a0":[["V",160],["S",96]],"a256":[["S",256]],"b0":[["V",192],["S",64]],"b256":[["S",256]],"a512":[["V",256]],"a768":[["V",224],["S",32]],"b512":[["V",64],["S",192]],"b768":[["S",256]],"c0":[["S",256]],"c256":[["V",96],["S",32]],"c384":[["S",128]],"d0":[["S",256]],"d256":[["S",128]],"d384":[["V",128]]}
STAGES = ["d0","b1","a0","c0","b0","x","a1","h0","h1","c1","d1","d2","c2"]
H_GROUP = [4,2]
X_QUANT = [[0,512],[512,256],[768,256]]
W2_QUANT = [[0,256],[256,128],[384,128]]
L2 = [[[0,1,2,"S"]],[[1,0,2,"S"]],[[1,1,2,"V"]],[[0,0,2,"S"]],[[2,0,2,"S"]],[[2,1,2,"V"]],[[3,0,2,"V"]],[[3,1,2,"S"]]]
G_STEP = 256


def tile_picked_pick_glu_relu_srt_e_kernel(tc, xT, w1, w3, w2, offs, out):
    nc = tc.nc

    def copy(engine, dst, src):
        if engine == "V":
            nc.vector.tensor_copy(out=dst, in_=src)
        elif engine == "S":
            nc.scalar.copy(out=dst, in_=src)
        else:
            nc.gpsimd.tensor_scalar(out=dst, in0=src, scalar1=1.0, scalar2=0.0, op0=MULT, op1=ADD)

    with ExitStack() as ctx:
        keep = ctx.enter_context(tc.tile_pool(name="keep", bufs=1))
        psum = ctx.enter_context(tc.psum_pool(name="psum", bufs=8))

        offsets = keep.tile([P, S // 16], U16, name="offsets")
        sources = {
            "x": xT.rearrange("(p j) w -> p j w", j=J),
            "a": w1.rearrange("(p j) w -> p j w", j=J),
            "b": w3.rearrange("(p j) w -> p j w", j=J),
            "c": w2[:KP, :].rearrange("(p j) w -> p j w", j=J),
            "d": w2[KP:, :].rearrange("(p j) w -> p j w", j=J),
        }
        raws = {}
        for i, (key, first, width) in enumerate(ORDER):
            raw = keep.tile([P, J, width], F32, name=f"raw_{key}_{first}")
            nc.sync.dma_start(out=raw[:], in_=sources[key][:, :, first : first + width])
            for sub in range(0, width, 128):
                raws[(key, first + sub)] = (raw, sub)
            if i == 0:
                nc.sync.dma_start(offsets[:], offs)

        x_codes = keep.tile([P, T], U32, name="x_codes", align_bytes=64)
        x_scales = keep.tile([P, T], U8, name="x_scales", align_bytes=64)
        nc.gpsimd.memset(x_scales[:], 0)
        xg_codes = keep.tile([P, S], U32, name="xg_codes", align_bytes=64)
        xg_scales = keep.tile([P, S], U8, name="xg_scales", align_bytes=64)

        def shares(key, first):
            found = []
            a = 0
            for engine, n in SPLIT[f"{key}{first}"]:
                step = G_STEP if engine == "G" else n
                for s in range(0, n, step):
                    found.append((engine, a + s, a + min(s + step, n)))
                a += n
            return found

        def plain_casts(key, first, grouped):
            for engine, a, b in shares(key, first):
                raw, sub = raws[(key, first)]
                copy(
                    engine,
                    grouped[:, a:b, :].rearrange("p (c i) j -> p c j i", i=4),
                    raw[:, :, sub + a : sub + b].rearrange("p j (c i) -> p c j i", i=4),
                )

        def tokens():
            for first, width in X_QUANT:
                grouped = keep.tile([P, width, J], BF16, name=f"x_grouped{first}", align_bytes=64)
                for sub in range(0, width, Q):
                    plain_casts("x", first + sub, grouped[:, sub : sub + Q, :])
                nc.vector.quantize_mx(
                    out=x_codes[:, first : first + width].bitcast(FP8X4),
                    scales=x_scales[:, first : first + width],
                    in_=grouped[:].rearrange("p w j -> p (w j)"),
                )
            nc.vector.tensor_copy(xg_codes[:], x_codes[:].indirect(offsets[:]))
            nc.vector.tensor_copy(xg_scales[:], x_scales[:].indirect(offsets[:]))

        w_codes = {}
        w_scales = {}

        def first_weights(w, c):
            grouped = keep.tile([P, J, P, J], BF16, name=f"w_grouped_{w}{c}", align_bytes=64)
            codes = keep.tile([P, KP], U32, name=f"w_codes_{w}{c}", align_bytes=64)
            scales = keep.tile([P, KP], U8, name=f"w_scales_{w}{c}", align_bytes=64)
            for sub in (0, Q):
                raw, at = raws[(w, c * KP + sub)]
                m0 = sub // 4
                for engine, a, b in shares(w, c * KP + sub):
                    copy(
                        engine,
                        grouped[:, :, m0 + a // 4 : m0 + b // 4, :].rearrange("p t m j -> p m t j"),
                        raw[:, :, at + a : at + b].rearrange("p j (m t) -> p m t j", t=4),
                    )
            nc.vector.quantize_mx(
                out=codes[:].bitcast(FP8X4), scales=scales[:], in_=grouped[:].rearrange("p t m j -> p (t m j)")
            )
            w_codes[(w, c)] = codes
            w_scales[(w, c)] = scales

        h_codes = {}
        h_scales = {}

        def products(w, c, b):
            cols = slice(b * NB, (b + 1) * NB)
            bank = psum.tile([P, J, NB], F32, name="bank", tag="bank")
            for t in range(J):
                rows = slice(t * P, (t + 1) * P)
                nc.tensor.matmul_mx(
                    out=bank[:, t, :],
                    lhsT=w_codes[(w, c)][:, rows].bitcast(FP8X4),
                    lhsT_scale=w_scales[(w, c)][:, rows],
                    rhs=xg_codes[:, cols].bitcast(FP8X4),
                    rhs_scale=xg_scales[:, cols],
                    start=True,
                    stop=True,
                )
            return bank[:].rearrange("p t n -> p n t")

        def first_layer(c):
            grouped = keep.tile([P, S, J], BF16, name=f"h_grouped{c}", align_bytes=64)
            codes = keep.tile([P, S], U32, name=f"h_codes{c}", align_bytes=64)
            scales = keep.tile([P, S], U8, name=f"h_scales{c}", align_bytes=64)
            gates = []
            for b in range(S // NB):
                gate = keep.tile([P, NB, J], F32, name=f"gate{c}_{b}")
                nc.scalar.activation(gate[:], products("a", c, b), RELU)
                gates.append(gate)
            for b in range(S // NB):
                up = products("b", c, b)
                nc.vector.tensor_tensor(
                    out=grouped[:, b * NB : (b + 1) * NB, :], in0=gates[b][:], in1=up, op=MULT
                )
                if (b + 1) % H_GROUP[c] == 0:
                    cols = slice((b + 1 - H_GROUP[c]) * NB, (b + 1) * NB)
                    nc.vector.quantize_mx(
                        out=codes[:, cols].bitcast(FP8X4),
                        scales=scales[:, cols],
                        in_=grouped[:, cols, :].rearrange("p n j -> p (n j)"),
                    )
            h_codes[c] = codes
            h_scales[c] = scales

        w2_codes = {}
        w2_scales = {}

        def second_weights(key, piece):
            first, width = W2_QUANT[piece]
            grouped = keep.tile([P, width, J], BF16, name=f"w2_grouped_{key}{piece}", align_bytes=64)
            codes = keep.tile([P, width], U32, name=f"w2_codes_{key}{piece}", align_bytes=64)
            scales = keep.tile([P, width], U8, name=f"w2_scales_{key}{piece}", align_bytes=64)
            plain_casts(key, first, grouped)
            nc.vector.quantize_mx(
                out=codes[:].bitcast(FP8X4), scales=scales[:], in_=grouped[:].rearrange("p m j -> p (m j)")
            )
            for m in range(0, width, P):
                w2_codes[(key, (first + m) // P)] = codes[:, m : m + P]
                w2_scales[(key, (first + m) // P)] = scales[:, m : m + P]

        for stage in STAGES:
            if stage == "x":
                tokens()
            elif stage[0] in "ab":
                first_weights(stage[0], int(stage[1]))
            elif stage[0] == "h":
                first_layer(int(stage[1]))
            else:
                second_weights(stage[0], int(stage[1]))

        for group in L2:
            banks = []
            for m, th, parts, engine in group:
                bank = psum.tile([P, S // parts], F32, name="bank", tag="bank")
                banks.append(bank)
            for c, key in enumerate("cd"):
                for bank, (m, th, parts, engine) in zip(banks, group):
                    cols = slice(th * (S // parts), (th + 1) * (S // parts))
                    nc.tensor.matmul_mx(
                        out=bank[:],
                        lhsT=w2_codes[(key, m)].bitcast(FP8X4),
                        lhsT_scale=w2_scales[(key, m)],
                        rhs=h_codes[c][:, cols].bitcast(FP8X4),
                        rhs_scale=h_scales[c][:, cols],
                        start=(c == 0),
                        stop=(c == 1),
                    )
            for bank, (m, th, parts, engine) in zip(banks, group):
                cols = slice(th * (S // parts), (th + 1) * (S // parts))
                result = keep.tile([P, S // parts], F32, name=f"result{m}_{th}")
                copy(engine, result[:], bank[:])
                nc.sync.dma_start(out=out[m * P : (m + 1) * P, cols], in_=result[:])
